import numpy as np
import ml_dtypes


def mxq(x, axis, fmt="e4m3"):
    dtype, down = {"e4m3": (ml_dtypes.float8_e4m3fn, 7), "e5m2": (ml_dtypes.float8_e5m2, 14)}[fmt]
    v = np.moveaxis(np.asarray(x, np.float32).astype(ml_dtypes.bfloat16).astype(np.float64), axis, -1)
    blocks = v.reshape(v.shape[:-1] + (-1, 32))
    amax = np.abs(blocks).max(-1, keepdims=True)
    byte = np.maximum(np.where(amax > 0, np.frexp(amax)[1] - 1 + 127, 0) - down, 1)
    scale = np.exp2(byte - 127.0)
    codes = (blocks / scale).astype(np.float32).astype(dtype).astype(np.float64)
    return np.moveaxis((codes * scale).reshape(v.shape), -1, axis)


WIDE = False


def mx_kscale(k):
    if not WIDE:
        return np.ones(k)
    levels = np.array([10, -10, 5, -5, 0])
    if k % 512:
        return np.exp2(np.random.permutation(np.resize(levels, k // 32))).repeat(32)
    a = np.empty((k // 512, 16))
    for p in range(k // 512):
        a[p, :8] = np.random.permutation(np.resize(levels, 8))
        for g in range(8):
            far = levels[np.abs(levels - a[p, g]) >= 10]
            a[p, g + 8] = far[np.random.randint(len(far))]
    return np.exp2(a.ravel()).repeat(32)


def f64(x):
    return np.asarray(x).astype(np.float64)


def striped8(idx):
    return np.concatenate([v.reshape(-1, 16).T for v in idx]).astype(np.uint16)


def unstriped8(offs):
    return np.stack([offs[16 * g:16 * g + 16].T.reshape(-1) for g in range(8)]).astype(np.int64)


E2M1 = np.array([0.0, 0.5, 1.0, 1.5, 2.0, 3.0, 4.0, 6.0, -0.0, -0.5, -1.0, -1.5, -2.0, -3.0, -4.0, -6.0])


def pack_weight(w, fmt):
    k, n = w.shape
    w = f64(np.asarray(w, np.float32).astype(ml_dtypes.bfloat16)).reshape(k // 32, 32, n)
    amax = np.abs(w).max(1)
    if fmt == "e4m3":
        byte = np.frexp(amax)[1] - 1 + 127 - 7
    else:
        mant, ex = np.frexp(amax / 6.0)
        byte = np.where(mant > 0.5, ex, ex - 1) + 127
    byte = np.clip(np.where(amax > 0, byte, 1), 1, 254)
    scaled = (w * np.exp2(127.0 - byte)[:, None, :]).reshape(k, n).astype(np.float32)
    by_word = np.ascontiguousarray(scaled.reshape(k // 512, 128, 4, n).transpose(0, 1, 3, 2))
    if fmt == "e4m3":
        words = by_word.astype(ml_dtypes.float8_e4m3fn).view(np.uint8)
    else:
        c = by_word.astype(ml_dtypes.float4_e2m1fn).view(np.uint8) & 0xF
        words = (c[..., 0::2] | (c[..., 1::2] << 4)).reshape(k // 512, 128, 2 * n)
    return np.ascontiguousarray(words), np.ascontiguousarray(byte.astype(np.uint8).reshape(k // 512, 16, n))


def unpack_weight(words, scales, fmt):
    g, _, n = scales.shape
    words = np.ascontiguousarray(words).reshape(g, 128, n, -1)
    if fmt == "e4m3":
        vals = words.view(ml_dtypes.float8_e4m3fn).astype(np.float64)
    else:
        nib = np.empty((g, 128, n, 4), np.uint8)
        nib[..., 0::2] = words & 0xF
        nib[..., 1::2] = words >> 4
        vals = E2M1[nib]
    vals = vals * np.repeat(np.exp2(scales.astype(np.float64) - 127.0), 8, axis=1)[..., None]
    return vals.transpose(0, 1, 3, 2).reshape(g * 512, n)


K, R, M, T, S = 2048, 512, 1536, 1024, 512


def setup_inputs():
    n = np.random.standard_normal
    s = mx_kscale(K)[:, None]
    u = mx_kscale(R)[:, None]
    p_w4 = pack_weight(n((K, M)) / np.sqrt(K) / s, "e2m1")
    return {
        "xT": (n((K, T)) * s).astype(np.float32),
        "w4_words": p_w4[0],
        "w4_scales": p_w4[1],
        "down": (n((K, R)) / np.sqrt(K) / s * u.T).astype(np.float32),
        "up": (0.5 * n((R, M)) / np.sqrt(R) / u).astype(np.float32),
        "wgt": np.repeat(np.random.uniform(0.5, 2.0, (8, S)), 16, axis=0).astype(np.float32),
        "b": (0.3 * n(1536)).astype(np.float32),
        "offs": striped8(np.stack([np.random.permutation(T)[:S] for _ in range(8)])),
    }


def reference(xT, w4_words, w4_scales, down, up, wgt, b, offs):
    idx = unstriped8(offs)
    group = np.arange(K) % 512 // 64
    xg = f64(wgt)[np.arange(K) // 4 % 128] * f64(xT)[np.arange(K)[:, None], idx[group]]
    xT_ = mxq(xg, 0, "e4m3")
    w4_ = unpack_weight(w4_words, w4_scales, "e2m1")
    down_ = mxq(f64(down), 0, "e4m3")
    up_ = mxq(f64(up), 0, "e4m3")
    h_ = mxq(down_.T @ xT_, 0, "e4m3")
    y = w4_.T @ xT_ + up_.T @ h_
    return y + f64(b)[:, None]

@@ -1,0 +1,255 @@
+from contextlib import ExitStack
+
+import concourse.mybir as mybir
+from concourse.masks import make_identity
+
+F32 = mybir.dt.float32
+BF16 = mybir.dt.bfloat16
+I32 = mybir.dt.int32
+U32 = mybir.dt.uint32
+U16 = mybir.dt.uint16
+U8 = mybir.dt.uint8
+E4M3 = mybir.dt.float8_e4m3fn_x4
+E2M1 = mybir.dt.float4_e2m1fn_x4
+ADD = mybir.AluOpType.add
+MULT = mybir.AluOpType.mult
+IDENTITY = mybir.ActivationFunctionType.Identity
+
+P = 128
+K, R, M, T, S = 2048, 512, 1536, 1024, 512
+PASSES = K // 512
+M_TILES = M // P
+ON_SCALAR = (0, 2, 4, 6, 8, 10)
+EARLY = 4
+
+FLOPS = 2 * S * (K * M + K * R + R * M)
+
+
+def tile_list_hlora_bias_kernel(tc, xT, w4_words, w4_scales, down, up, wgt, b, offs, out):
+    nc = tc.nc
+    with ExitStack() as ctx:
+        keep = ctx.enter_context(tc.tile_pool(name="keep", bufs=1))
+        stage = ctx.enter_context(tc.tile_pool(name="stage", bufs=2))
+        outs = ctx.enter_context(tc.tile_pool(name="outs", bufs=4))
+        psum = ctx.enter_context(tc.psum_pool(name="psum", bufs=1))
+
+        def bank(n):
+            return psum.tile([P, S], F32, name=f"bank{n}")
+
+        lists = keep.tile([P, S // 16], U16, name="lists")
+        nc.sync.dma_start(lists[:], offs)
+
+        w4_planes = keep.tile([P, PASSES, M], U8, name="w4_planes", align_bytes=64)
+        nc.vector.memset(w4_planes[:].rearrange("p a n -> p (a n)").bitcast(I32), 0)
+        for q in range(4):
+            nc.scalar.dma_start(
+                out=w4_planes[32 * q : 32 * q + 4, :, :].bitcast(I32),
+                in_=w4_scales[:, 4 * q : 4 * q + 4, :].rearrange("a q n -> q a n").bitcast(I32),
+            )
+        b_rows = keep.tile([P, P], F32, name="b_rows")
+        nc.gpsimd.memset(b_rows[:], 0.0)
+        b_lines = b.rearrange("(m p) -> m p", p=P)
+        nc.scalar.dma_start(out=b_rows[0:8, :], in_=b_lines[0:8, :])
+        nc.scalar.dma_start(out=b_rows[8:12, :], in_=b_lines[8:12, :])
+        ident = keep.tile([P, P], F32, name="ident")
+        make_identity(nc, ident[:])
+
+        weight = keep.tile([P, S], F32, name="weight")
+        windows = {}
+        down_raw = {}
+        up_raw = {}
+        w4_early = keep.tile([P, PASSES, 2 * P * EARLY], U8, name="w4_early", align_bytes=64)
+        w4_late = keep.tile([P, PASSES, 2 * (M - P * EARLY)], U8, name="w4_late", align_bytes=64)
+
+        def load_plane(a, i):
+            windows[a, i] = keep.tile([P, T], F32, name=f"win{a}_{i}")
+            nc.sync.dma_start(windows[a, i][:], xT[512 * a : 512 * (a + 1), :].rearrange("(p i) t -> p i t", i=4)[:, i, :])
+
+        def load_down(a):
+            down_raw[a] = keep.tile([P, 4, R], F32, name=f"down_raw{a}")
+            nc.sync.dma_start(down_raw[a][:], down[512 * a : 512 * (a + 1), :].rearrange("(p j) r -> p j r", j=4))
+
+        def load_up(c):
+            up_raw[c] = keep.tile([P, 4, 512], F32, name=f"up_raw{c}")
+            nc.sync.dma_start(up_raw[c][:], up[:, 512 * c : 512 * (c + 1)].rearrange("(p j) n -> p j n", j=4))
+
+        def load_w4(tile, first, last):
+            nc.sync.dma_start(
+                tile[:].bitcast(I32),
+                w4_words[:, :, 2 * P * first : 2 * P * last].rearrange("a p n -> p a n").bitcast(I32),
+            )
+
+        load_plane(0, 0)
+        nc.sync.dma_start(weight[:], wgt)
+        for i in range(1, 4):
+            load_plane(0, i)
+        load_down(0)
+        for i in range(4):
+            load_plane(1, i)
+        load_down(1)
+        for i in range(4):
+            load_plane(2, i)
+        load_w4(w4_early, 0, EARLY)
+        for i in range(4):
+            load_plane(3, i)
+        load_down(2)
+        load_down(3)
+        load_w4(w4_late, EARLY, M_TILES)
+        load_up(0)
+        load_up(1)
+        load_up(2)
+
+        b_ps = bank(0)
+        nc.tensor.transpose(b_ps[:, 0:P], b_rows[:], ident[:])
+        b_col = keep.tile([P, M_TILES], F32, name="b_col")
+        nc.vector.tensor_copy(b_col[:], b_ps[:, 0:M_TILES])
+
+        def quantised(name, width):
+            codes = keep.tile([P, width], U32, name=f"{name}_codes", align_bytes=64)
+            plane = keep.tile([P, width], U8, name=f"{name}_plane", align_bytes=64)
+            return codes, plane
+
+        def quantise(pair, grouped, c0, c1):
+            codes, plane = pair
+            nc.vector.quantize_mx(
+                out=codes[:, c0:c1].bitcast(E4M3), scales=plane[:, c0:c1], in_=grouped[:, 4 * c0 : 4 * c1]
+            )
+
+        def interleave(copy, grouped, planes, c0, c1):
+            copy(
+                out=grouped[:, 4 * c0 : 4 * c1].rearrange("p (c i t) -> p c t i", i=4, t=4),
+                in_=planes[:, :, c0:c1].rearrange("p t (c i) -> p c t i", i=4),
+            )
+
+        xg = {}
+
+        def both(function, lo, mid, hi):
+            if mid > lo:
+                function(nc.vector.tensor_copy, lo, mid)
+            if hi > mid:
+                function(nc.scalar.copy, mid, hi)
+
+        def pick(a, share):
+            picked = stage.tile([P, 4, S], F32, name="picked")
+            for i in range(4):
+                for h in range(2):
+                    cols = slice(256 * h, 256 * (h + 1))
+                    nc.vector.tensor_tensor(
+                        out=picked[:, i, cols],
+                        in0=windows[a, i][:].indirect(lists[:, 16 * h : 16 * (h + 1)]),
+                        in1=weight[:, cols],
+                        op=MULT,
+                    )
+            grouped = stage.tile([P, 4 * S], BF16, name="xg_grouped", align_bytes=64)
+            both(lambda copy, c0, c1: interleave(copy, grouped, picked, c0, c1), 0, share, S)
+            xg[a] = quantised(f"xg{a}", S)
+            quantise(xg[a], grouped, 0, S)
+
+        def w4_pass(m, a):
+            tile, mm = (w4_early, m) if m < EARLY else (w4_late, m - EARLY)
+            nc.tensor.matmul_mx(
+                out=y[m][:],
+                lhsT=tile[:, a, 2 * P * mm : 2 * P * (mm + 1)].bitcast(E2M1),
+                lhsT_scale=w4_planes[:, a, P * m : P * (m + 1)],
+                rhs=xg[a][0][:].bitcast(E4M3),
+                rhs_scale=xg[a][1][:],
+                start=(a == 0),
+                stop=False,
+            )
+
+        def down_group(copy, grouped, raw, m0, m1):
+            copy(
+                out=grouped[:].rearrange("p (t m j) -> p m j t", t=4, j=4)[:, m0:m1, :, :],
+                in_=raw[:].rearrange("p j (m t) -> p m j t", t=4)[:, m0:m1, :, :],
+            )
+
+        def h_passes(a, share):
+            grouped = stage.tile([P, 4 * R], BF16, name="down_grouped", align_bytes=64)
+            both(lambda copy, m0, m1: down_group(copy, grouped, down_raw[a], m0, m1), 0, share, P)
+            pair = quantised(f"down{a}", R)
+            quantise(pair, grouped, 0, R)
+            for t in range(4):
+                nc.tensor.matmul_mx(
+                    out=h_acc[t][:],
+                    lhsT=pair[0][:, P * t : P * (t + 1)].bitcast(E4M3),
+                    lhsT_scale=pair[1][:, P * t : P * (t + 1)],
+                    rhs=xg[a][0][:].bitcast(E4M3),
+                    rhs_scale=xg[a][1][:],
+                    start=(a == 0),
+                    stop=(a == PASSES - 1),
+                )
+
+        up_pairs = {}
+
+        def prepare_up(c, share):
+            grouped = stage.tile([P, 4 * 512], BF16, name="up_grouped", align_bytes=64)
+            both(lambda copy, c0, c1: interleave(copy, grouped, up_raw[c], c0, c1), 0, share, 512)
+            up_pairs[c] = quantised(f"up{c}", 512)
+            quantise(up_pairs[c], grouped, 0, 512)
+
+        h_planes = keep.tile([P, 4, S], BF16, name="h_planes", align_bytes=64)
+        h_grouped = keep.tile([P, 4 * S], BF16, name="h_grouped", align_bytes=64)
+        h = quantised("h", S)
+
+        def finish_h(share):
+            for t in range(4):
+                copy = nc.scalar.copy if t % 2 == 0 else nc.vector.tensor_copy
+                copy(out=h_planes[:, t, :], in_=h_acc[t][:])
+            both(lambda copy, c0, c1: interleave(copy, h_grouped, h_planes, c0, c1), 0, share, S)
+            quantise(h, h_grouped, 0, 256)
+            quantise(h, h_grouped, 256, 512)
+
+        def finish(m):
+            codes, plane = up_pairs[m // 4]
+            cols = slice(P * (m % 4), P * (m % 4 + 1))
+            nc.tensor.matmul_mx(
+                out=y[m][:],
+                lhsT=codes[:, cols].bitcast(E4M3),
+                lhsT_scale=plane[:, cols],
+                rhs=h[0][:].bitcast(E4M3),
+                rhs_scale=h[1][:],
+                start=False,
+                stop=True,
+            )
+            result = outs.tile([P, S], F32, name="result")
+            if m in ON_SCALAR:
+                nc.scalar.activation(result[:], y[m][:], IDENTITY, bias=b_col[:, m : m + 1])
+            else:
+                nc.vector.tensor_scalar(out=result[:], in0=y[m][:], scalar1=b_col[:, m : m + 1], scalar2=None, op0=ADD)
+            nc.sync.dma_start(out[P * m : P * (m + 1), :], result[:])
+
+        y = {m: bank(4 + m) for m in range(EARLY)}
+        h_acc = [bank(t) for t in range(4)]
+        pick(0, 0)
+        h_passes(0, 0)
+        pick(1, 0)
+        h_passes(1, 0)
+        pick(2, 0)
+        pick(3, 0)
+        for m in range(EARLY):
+            w4_pass(m, 0)
+        for m in range(EARLY):
+            w4_pass(m, 1)
+        for m in range(EARLY):
+            w4_pass(m, 2)
+        for m in range(EARLY):
+            w4_pass(m, 3)
+        h_passes(2, 128)
+        h_passes(3, 80)
+        finish_h(256)
+        for m in range(4, 8):
+            y[m] = bank(m - 4)
+            for a in range(PASSES):
+                w4_pass(m, a)
+        prepare_up(0, 384)
+        for m in range(0, 4):
+            finish(m)
+        prepare_up(1, 256)
+        for m in range(4, 8):
+            finish(m)
+        prepare_up(2, 256)
+        for m in range(8, 12):
+            y[m] = bank(m - 4)
+            for a in range(PASSES):
+                w4_pass(m, a)
+            finish(m)

@@ -19,7 +19,7 @@ P = 128
 K, R, M, T, S = 2048, 512, 1536, 1024, 512
 PASSES = K // 512
 M_TILES = M // P
-ON_SCALAR = (0, 2, 4, 6, 8, 10)
+ON_VECTOR = (2, 6, 9)
 EARLY = 4
 
 FLOPS = 2 * S * (K * M + K * R + R * M)
@@ -37,7 +37,6 @@ def tile_list_hlora_bias_kernel(tc, xT, w4_words, w4_scales, down, up, wgt, b, o
             return psum.tile([P, S], F32, name=f"bank{n}")
 
         lists = keep.tile([P, S // 16], U16, name="lists")
-        nc.sync.dma_start(lists[:], offs)
 
         w4_planes = keep.tile([P, PASSES, M], U8, name="w4_planes", align_bytes=64)
         nc.vector.memset(w4_planes[:].rearrange("p a n -> p (a n)").bitcast(I32), 0)
@@ -79,23 +78,20 @@ def tile_list_hlora_bias_kernel(tc, xT, w4_words, w4_scales, down, up, wgt, b, o
                 w4_words[:, :, 2 * P * first : 2 * P * last].rearrange("a p n -> p a n").bitcast(I32),
             )
 
-        load_plane(0, 0)
         nc.sync.dma_start(weight[:], wgt)
-        for i in range(1, 4):
-            load_plane(0, i)
+        nc.sync.dma_start(lists[:], offs)
+        for a in range(3):
+            for i in range(4):
+                load_plane(a, i)
         load_down(0)
         for i in range(4):
-            load_plane(1, i)
-        load_down(1)
-        for i in range(4):
-            load_plane(2, i)
-        load_w4(w4_early, 0, EARLY)
-        for i in range(4):
             load_plane(3, i)
+        load_down(1)
+        load_w4(w4_early, 0, EARLY)
         load_down(2)
         load_down(3)
-        load_w4(w4_late, EARLY, M_TILES)
         load_up(0)
+        load_w4(w4_late, EARLY, M_TILES)
         load_up(1)
         load_up(2)
 
@@ -121,7 +117,7 @@ def tile_list_hlora_bias_kernel(tc, xT, w4_words, w4_scales, down, up, wgt, b, o
                 in_=planes[:, :, c0:c1].rearrange("p t (c i) -> p c t i", i=4),
             )
 
-        xg = {}
+        xg, x_grouped, down_pairs, w_grouped, up_pairs = {}, {}, {}, {}, {}
 
         def both(function, lo, mid, hi):
             if mid > lo:
@@ -129,8 +125,8 @@ def tile_list_hlora_bias_kernel(tc, xT, w4_words, w4_scales, down, up, wgt, b, o
             if hi > mid:
                 function(nc.scalar.copy, mid, hi)
 
-        def pick(a, share):
-            picked = stage.tile([P, 4, S], F32, name="picked")
+        def pick(a):
+            picked = stage.tile([P, 4, S], F32, name="picked", bufs=2)
             for i in range(4):
                 for h in range(2):
                     cols = slice(256 * h, 256 * (h + 1))
@@ -140,64 +136,61 @@ def tile_list_hlora_bias_kernel(tc, xT, w4_words, w4_scales, down, up, wgt, b, o
                         in1=weight[:, cols],
                         op=MULT,
                     )
-            grouped = stage.tile([P, 4 * S], BF16, name="xg_grouped", align_bytes=64)
-            both(lambda copy, c0, c1: interleave(copy, grouped, picked, c0, c1), 0, share, S)
+            x_grouped[a] = stage.tile([P, 4 * S], BF16, name="x_grouped", align_bytes=64, bufs=3)
+            interleave(nc.scalar.copy, x_grouped[a], picked, 0, S)
+
+        def quantise_x(a):
             xg[a] = quantised(f"xg{a}", S)
-            quantise(xg[a], grouped, 0, S)
+            quantise(xg[a], x_grouped[a], 0, S)
 
-        def w4_pass(m, a):
-            tile, mm = (w4_early, m) if m < EARLY else (w4_late, m - EARLY)
-            nc.tensor.matmul_mx(
-                out=y[m][:],
-                lhsT=tile[:, a, 2 * P * mm : 2 * P * (mm + 1)].bitcast(E2M1),
-                lhsT_scale=w4_planes[:, a, P * m : P * (m + 1)],
-                rhs=xg[a][0][:].bitcast(E4M3),
-                rhs_scale=xg[a][1][:],
-                start=(a == 0),
-                stop=False,
-            )
+        def w4_passes(a, tiles):
+            for m in tiles:
+                tile, mm = (w4_early, m) if m < EARLY else (w4_late, m - EARLY)
+                nc.tensor.matmul_mx(
+                    out=y[m][:],
+                    lhsT=tile[:, a, 2 * P * mm : 2 * P * (mm + 1)].bitcast(E2M1),
+                    lhsT_scale=w4_planes[:, a, P * m : P * (m + 1)],
+                    rhs=xg[a][0][:].bitcast(E4M3),
+                    rhs_scale=xg[a][1][:],
+                    start=(a == 0),
+                    stop=False,
+                )
 
-        def down_group(copy, grouped, raw, m0, m1):
-            copy(
-                out=grouped[:].rearrange("p (t m j) -> p m j t", t=4, j=4)[:, m0:m1, :, :],
-                in_=raw[:].rearrange("p j (m t) -> p m j t", t=4)[:, m0:m1, :, :],
-            )
+        def group_down(a, share):
+            w_grouped[a] = stage.tile([P, 4 * R], BF16, name="w_grouped", align_bytes=64, bufs=3)
 
-        def h_passes(a, share):
-            grouped = stage.tile([P, 4 * R], BF16, name="down_grouped", align_bytes=64)
-            both(lambda copy, m0, m1: down_group(copy, grouped, down_raw[a], m0, m1), 0, share, P)
-            pair = quantised(f"down{a}", R)
-            quantise(pair, grouped, 0, R)
+            def part(copy, m0, m1):
+                copy(
+                    out=w_grouped[a][:].rearrange("p (t m j) -> p m j t", t=4, j=4)[:, m0:m1, :, :],
+                    in_=down_raw[a][:].rearrange("p j (m t) -> p m j t", t=4)[:, m0:m1, :, :],
+                )
+
+            both(part, 0, share, P)
+
+        def quantise_down(a):
+            down_pairs[a] = quantised(f"down{a}", R)
+            quantise(down_pairs[a], w_grouped[a], 0, R)
+
+        def h_passes(a):
+            codes, plane = down_pairs[a]
             for t in range(4):
                 nc.tensor.matmul_mx(
                     out=h_acc[t][:],
-                    lhsT=pair[0][:, P * t : P * (t + 1)].bitcast(E4M3),
-                    lhsT_scale=pair[1][:, P * t : P * (t + 1)],
+                    lhsT=codes[:, P * t : P * (t + 1)].bitcast(E4M3),
+                    lhsT_scale=plane[:, P * t : P * (t + 1)],
                     rhs=xg[a][0][:].bitcast(E4M3),
                     rhs_scale=xg[a][1][:],
                     start=(a == 0),
                     stop=(a == PASSES - 1),
                 )
 
-        up_pairs = {}
+        def group_up(c, share):
+            w_grouped["up", c] = stage.tile([P, 4 * 512], BF16, name="w_grouped", align_bytes=64, bufs=3)
+            both(lambda copy, c0, c1: interleave(copy, w_grouped["up", c], up_raw[c], c0, c1), 0, share, 512)
 
-        def prepare_up(c, share):
-            grouped = stage.tile([P, 4 * 512], BF16, name="up_grouped", align_bytes=64)
-            both(lambda copy, c0, c1: interleave(copy, grouped, up_raw[c], c0, c1), 0, share, 512)
+        def quantise_up(c):
             up_pairs[c] = quantised(f"up{c}", 512)
-            quantise(up_pairs[c], grouped, 0, 512)
-
-        h_planes = keep.tile([P, 4, S], BF16, name="h_planes", align_bytes=64)
-        h_grouped = keep.tile([P, 4 * S], BF16, name="h_grouped", align_bytes=64)
-        h = quantised("h", S)
-
-        def finish_h(share):
-            for t in range(4):
-                copy = nc.scalar.copy if t % 2 == 0 else nc.vector.tensor_copy
-                copy(out=h_planes[:, t, :], in_=h_acc[t][:])
-            both(lambda copy, c0, c1: interleave(copy, h_grouped, h_planes, c0, c1), 0, share, S)
-            quantise(h, h_grouped, 0, 256)
-            quantise(h, h_grouped, 256, 512)
+            quantise(up_pairs[c], w_grouped["up", c], 0, 512)
 
         def finish(m):
             codes, plane = up_pairs[m // 4]
@@ -212,44 +205,73 @@ def tile_list_hlora_bias_kernel(tc, xT, w4_words, w4_scales, down, up, wgt, b, o
                 stop=True,
             )
             result = outs.tile([P, S], F32, name="result")
-            if m in ON_SCALAR:
-                nc.scalar.activation(result[:], y[m][:], IDENTITY, bias=b_col[:, m : m + 1])
-            else:
+            if m in ON_VECTOR:
                 nc.vector.tensor_scalar(out=result[:], in0=y[m][:], scalar1=b_col[:, m : m + 1], scalar2=None, op0=ADD)
+            else:
+                nc.scalar.activation(result[:], y[m][:], IDENTITY, bias=b_col[:, m : m + 1])
             nc.sync.dma_start(out[P * m : P * (m + 1), :], result[:])
+
+        def open_tiles(tiles):
+            for m in tiles:
+                y[m] = bank((m + 4) % 8)
+            for a in range(PASSES):
+                w4_passes(a, tiles)
 
         y = {m: bank(4 + m) for m in range(EARLY)}
         h_acc = [bank(t) for t in range(4)]
-        pick(0, 0)
-        h_passes(0, 0)
-        pick(1, 0)
-        h_passes(1, 0)
-        pick(2, 0)
-        pick(3, 0)
-        for m in range(EARLY):
-            w4_pass(m, 0)
-        for m in range(EARLY):
-            w4_pass(m, 1)
-        for m in range(EARLY):
-            w4_pass(m, 2)
-        for m in range(EARLY):
-            w4_pass(m, 3)
-        h_passes(2, 128)
-        h_passes(3, 80)
-        finish_h(256)
-        for m in range(4, 8):
-            y[m] = bank(m - 4)
-            for a in range(PASSES):
-                w4_pass(m, a)
-        prepare_up(0, 384)
-        for m in range(0, 4):
+        pick(0)
+        pick(1)
+        group_down(0, 0)
+        quantise_x(0)
+        w4_passes(0, range(EARLY))
+        pick(2)
+        quantise_x(1)
+        w4_passes(1, range(EARLY))
+        pick(3)
+        quantise_down(0)
+        h_passes(0)
+        quantise_x(2)
+        w4_passes(2, range(EARLY))
+        group_down(1, P)
+        quantise_down(1)
+        h_passes(1)
+        quantise_x(3)
+        group_down(2, P)
+        quantise_down(2)
+        h_passes(2)
+        group_down(3, 64)
+        quantise_down(3)
+        h_passes(3)
+        w4_passes(3, range(EARLY))
+
+        group_up(0, 384)
+        h_planes = keep.tile([P, 4, S], BF16, name="h_planes", align_bytes=64)
+        h_grouped = keep.tile([P, 4 * S], BF16, name="h_grouped", align_bytes=64)
+        for t in range(4):
+            copy = nc.vector.tensor_copy if t == 1 else nc.scalar.copy
+            copy(out=h_planes[:, t, :], in_=h_acc[t][:])
+        quantise_up(0)
+        both(lambda copy, c0, c1: interleave(copy, h_grouped, h_planes, c0, c1), 0, 256, 512)
+        h = quantised("h", S)
+        quantise(h, h_grouped, 0, 256)
+        quantise(h, h_grouped, 256, 512)
+        group_up(1, 512)
+        open_tiles((4, 5))
+        for m in range(4):
             finish(m)
-        prepare_up(1, 256)
-        for m in range(4, 8):
-            finish(m)
-        prepare_up(2, 256)
-        for m in range(8, 12):
-            y[m] = bank(m - 4)
-            for a in range(PASSES):
-                w4_pass(m, a)
-            finish(m)
+        quantise_up(1)
+        group_up(2, 512)
+        open_tiles((6, 7))
+        finish(4)
+        finish(5)
+        open_tiles((8,))
+        finish(6)
+        open_tiles((9,))
+        finish(7)
+        quantise_up(2)
+        finish(8)
+        finish(9)
+        open_tiles((10,))
+        finish(10)
+        open_tiles((11,))
+        finish(11)

@@ -40,16 +40,16 @@ def tile_list_hlora_bias_kernel(tc, xT, w4_words, w4_scales, down, up, wgt, b, o
 
         w4_planes = keep.tile([P, PASSES, M], U8, name="w4_planes", align_bytes=64)
         nc.vector.memset(w4_planes[:].rearrange("p a n -> p (a n)").bitcast(I32), 0)
-        for q in range(4):
-            nc.scalar.dma_start(
-                out=w4_planes[32 * q : 32 * q + 4, :, :].bitcast(I32),
-                in_=w4_scales[:, 4 * q : 4 * q + 4, :].rearrange("a q n -> q a n").bitcast(I32),
-            )
         b_rows = keep.tile([P, P], F32, name="b_rows")
         nc.gpsimd.memset(b_rows[:], 0.0)
         b_lines = b.rearrange("(m p) -> m p", p=P)
-        nc.scalar.dma_start(out=b_rows[0:8, :], in_=b_lines[0:8, :])
-        nc.scalar.dma_start(out=b_rows[8:12, :], in_=b_lines[8:12, :])
+        nc.gpsimd.dma_start(out=b_rows[0:8, :], in_=b_lines[0:8, :])
+        nc.gpsimd.dma_start(out=b_rows[8:12, :], in_=b_lines[8:12, :])
+        for q in range(4):
+            nc.gpsimd.dma_start(
+                out=w4_planes[32 * q : 32 * q + 4, :, :].bitcast(I32),
+                in_=w4_scales[:, 4 * q : 4 * q + 4, :].rearrange("a q n -> q a n").bitcast(I32),
+            )
         ident = keep.tile([P, P], F32, name="ident")
         make_identity(nc, ident[:])
 
@@ -80,21 +80,21 @@ def tile_list_hlora_bias_kernel(tc, xT, w4_words, w4_scales, down, up, wgt, b, o
 
         nc.sync.dma_start(weight[:], wgt)
         nc.sync.dma_start(lists[:], offs)
-        for a in range(3):
+        for a in range(2):
             for i in range(4):
                 load_plane(a, i)
+        load_w4(w4_early, 0, EARLY)
+        for i in range(4):
+            load_plane(2, i)
         load_down(0)
         for i in range(4):
             load_plane(3, i)
-        load_down(1)
-        load_w4(w4_early, 0, EARLY)
-        load_down(2)
-        load_down(3)
+        for a in range(1, PASSES):
+            load_down(a)
         load_up(0)
         load_w4(w4_late, EARLY, M_TILES)
         load_up(1)
         load_up(2)
-
         b_ps = bank(0)
         nc.tensor.transpose(b_ps[:, 0:P], b_rows[:], ident[:])
         b_col = keep.tile([P, M_TILES], F32, name="b_col")
@@ -161,8 +161,8 @@ def tile_list_hlora_bias_kernel(tc, xT, w4_words, w4_scales, down, up, wgt, b, o
 
             def part(copy, m0, m1):
                 copy(
-                    out=w_grouped[a][:].rearrange("p (t m j) -> p m j t", t=4, j=4)[:, m0:m1, :, :],
-                    in_=down_raw[a][:].rearrange("p j (m t) -> p m j t", t=4)[:, m0:m1, :, :],
+                    out=w_grouped[a][:].rearrange("p (t m j) -> p m t j", t=4, j=4)[:, m0:m1, :, :],
+                    in_=down_raw[a][:].rearrange("p j (m t) -> p m t j", t=4)[:, m0:m1, :, :],
                 )
 
             both(part, 0, share, P)

@@ -15,12 +15,21 @@ ADD = mybir.AluOpType.add
 MULT = mybir.AluOpType.mult
 IDENTITY = mybir.ActivationFunctionType.Identity
 
-P = 128
 K, R, M, T, S = 2048, 512, 1536, 1024, 512
-PASSES = K // 512
+P = 128
+PACK = 4
+PASSES = K // (P * PACK)
 M_TILES = M // P
-ON_VECTOR = (2, 6, 9)
+HALF = S // 2
+
+BANKS = 8
 EARLY = 4
+UP_COLS = 512
+UP_TILES = UP_COLS // P
+
+X_ON_VECTOR = [0, 0, 0, HALF]
+DOWN_ON_VECTOR = [0, 0, 64, 64]
+UP_ON_VECTOR = 384
 
 FLOPS = 2 * S * (K * M + K * R + R * M)
 
@@ -29,119 +38,145 @@ def tile_list_hlora_bias_kernel(tc, xT, w4_words, w4_scales, down, up, wgt, b, o
     nc = tc.nc
     with ExitStack() as ctx:
         keep = ctx.enter_context(tc.tile_pool(name="keep", bufs=1))
-        stage = ctx.enter_context(tc.tile_pool(name="stage", bufs=2))
-        outs = ctx.enter_context(tc.tile_pool(name="outs", bufs=4))
+        stage = ctx.enter_context(tc.tile_pool(name="stage", bufs=3))
+        outs = ctx.enter_context(tc.tile_pool(name="outs", bufs=8))
         psum = ctx.enter_context(tc.psum_pool(name="psum", bufs=1))
 
         def bank(n):
             return psum.tile([P, S], F32, name=f"bank{n}")
 
-        lists = keep.tile([P, S // 16], U16, name="lists")
-
-        w4_planes = keep.tile([P, PASSES, M], U8, name="w4_planes", align_bytes=64)
-        nc.vector.memset(w4_planes[:].rearrange("p a n -> p (a n)").bitcast(I32), 0)
+        w4_plane = keep.tile([P, PASSES, M], U8, name="w4_plane", align_bytes=64)
+        nc.vector.memset(w4_plane[:].rearrange("p a n -> p (a n)").bitcast(I32), 0)
         b_rows = keep.tile([P, P], F32, name="b_rows")
         nc.gpsimd.memset(b_rows[:], 0.0)
         b_lines = b.rearrange("(m p) -> m p", p=P)
-        nc.gpsimd.dma_start(out=b_rows[0:8, :], in_=b_lines[0:8, :])
-        nc.gpsimd.dma_start(out=b_rows[8:12, :], in_=b_lines[8:12, :])
+        for first, last in ((0, 8), (8, M_TILES)):
+            nc.gpsimd.dma_start(out=b_rows[first:last, :], in_=b_lines[first:last, :])
         for q in range(4):
             nc.gpsimd.dma_start(
-                out=w4_planes[32 * q : 32 * q + 4, :, :].bitcast(I32),
-                in_=w4_scales[:, 4 * q : 4 * q + 4, :].rearrange("a q n -> q a n").bitcast(I32),
+                out=w4_plane[32 * q : 32 * q + 4, :, :].bitcast(I32),
+                in_=w4_scales[:, 4 * q : 4 * q + 4, :].rearrange("a e n -> e a n").bitcast(I32),
             )
         ident = keep.tile([P, P], F32, name="ident")
         make_identity(nc, ident[:])
 
         weight = keep.tile([P, S], F32, name="weight")
-        windows = {}
-        down_raw = {}
-        up_raw = {}
+        lists = keep.tile([P, S // 16], U16, name="lists")
+        windows, down_raw, up_raw = {}, {}, {}
         w4_early = keep.tile([P, PASSES, 2 * P * EARLY], U8, name="w4_early", align_bytes=64)
-        w4_late = keep.tile([P, PASSES, 2 * (M - P * EARLY)], U8, name="w4_late", align_bytes=64)
+        w4_late = keep.tile([P, PASSES, 2 * P * (M_TILES - EARLY)], U8, name="w4_late", align_bytes=64)
 
-        def load_plane(a, i):
-            windows[a, i] = keep.tile([P, T], F32, name=f"win{a}_{i}")
-            nc.sync.dma_start(windows[a, i][:], xT[512 * a : 512 * (a + 1), :].rearrange("(p i) t -> p i t", i=4)[:, i, :])
+        def load_window(a, i):
+            windows[a, i] = keep.tile([P, T], F32, name=f"window{a}_{i}", tag=f"window{a}_{i}", align_bytes=64)
+            rows = xT[P * PACK * a : P * PACK * (a + 1), :].rearrange("(p i) t -> p i t", i=PACK)
+            nc.sync.dma_start(windows[a, i][:], rows[:, i, :])
 
         def load_down(a):
-            down_raw[a] = keep.tile([P, 4, R], F32, name=f"down_raw{a}")
-            nc.sync.dma_start(down_raw[a][:], down[512 * a : 512 * (a + 1), :].rearrange("(p j) r -> p j r", j=4))
+            down_raw[a] = keep.tile([P, PACK, R], F32, name=f"down_raw{a}")
+            rows = down[P * PACK * a : P * PACK * (a + 1), :]
+            nc.sync.dma_start(down_raw[a][:], rows.rearrange("(p i) r -> p i r", i=PACK))
 
         def load_up(c):
-            up_raw[c] = keep.tile([P, 4, 512], F32, name=f"up_raw{c}")
-            nc.sync.dma_start(up_raw[c][:], up[:, 512 * c : 512 * (c + 1)].rearrange("(p j) n -> p j n", j=4))
+            up_raw[c] = keep.tile([P, PACK, UP_COLS], F32, name=f"up_raw{c}")
+            cols = up[:, UP_COLS * c : UP_COLS * (c + 1)]
+            nc.sync.dma_start(up_raw[c][:], cols.rearrange("(p i) n -> p i n", i=PACK))
 
         def load_w4(tile, first, last):
-            nc.sync.dma_start(
-                tile[:].bitcast(I32),
-                w4_words[:, :, 2 * P * first : 2 * P * last].rearrange("a p n -> p a n").bitcast(I32),
-            )
+            cols = w4_words[:, :, 2 * P * first : 2 * P * last]
+            nc.sync.dma_start(tile[:].bitcast(I32), cols.rearrange("a p n -> p a n").bitcast(I32))
 
         nc.sync.dma_start(weight[:], wgt)
         nc.sync.dma_start(lists[:], offs)
-        for a in range(2):
-            for i in range(4):
-                load_plane(a, i)
+        for a in range(PASSES):
+            for i in range(PACK):
+                if a >= 2 and i == 2:
+                    load_down(a - 2)
+                load_window(a, i)
         load_w4(w4_early, 0, EARLY)
-        for i in range(4):
-            load_plane(2, i)
-        load_down(0)
-        for i in range(4):
-            load_plane(3, i)
-        for a in range(1, PASSES):
-            load_down(a)
+        load_down(2)
+        load_down(3)
         load_up(0)
         load_w4(w4_late, EARLY, M_TILES)
         load_up(1)
         load_up(2)
-        b_ps = bank(0)
-        nc.tensor.transpose(b_ps[:, 0:P], b_rows[:], ident[:])
-        b_col = keep.tile([P, M_TILES], F32, name="b_col")
-        nc.vector.tensor_copy(b_col[:], b_ps[:, 0:M_TILES])
 
-        def quantised(name, width):
-            codes = keep.tile([P, width], U32, name=f"{name}_codes", align_bytes=64)
+        def quantised(name, width, after=None):
+            codes = keep.tile([P, width], U32, name=f"{name}_codes", tag=after or f"{name}_codes", align_bytes=64)
             plane = keep.tile([P, width], U8, name=f"{name}_plane", align_bytes=64)
             return codes, plane
 
         def quantise(pair, grouped, c0, c1):
             codes, plane = pair
             nc.vector.quantize_mx(
-                out=codes[:, c0:c1].bitcast(E4M3), scales=plane[:, c0:c1], in_=grouped[:, 4 * c0 : 4 * c1]
+                out=codes[:, c0:c1].bitcast(E4M3), scales=plane[:, c0:c1], in_=grouped[:, PACK * c0 : PACK * c1]
             )
 
-        def interleave(copy, grouped, planes, c0, c1):
+        def multiply(acc, weights, cols, moving, **flags):
+            codes, plane = weights
+            nc.tensor.matmul_mx(
+                out=acc[:],
+                lhsT=codes[:, cols].bitcast(E4M3),
+                lhsT_scale=plane[:, cols],
+                rhs=moving[0][:].bitcast(E4M3),
+                rhs_scale=moving[1][:],
+                **flags,
+            )
+
+        def shared(part, lo, mid, hi):
+            if mid > lo:
+                part(nc.vector.tensor_copy, lo, mid)
+            if hi > mid:
+                part(nc.scalar.copy, mid, hi)
+
+        def interleave(copy, grouped, raw, c0, c1):
             copy(
-                out=grouped[:, 4 * c0 : 4 * c1].rearrange("p (c i t) -> p c t i", i=4, t=4),
-                in_=planes[:, :, c0:c1].rearrange("p t (c i) -> p c t i", i=4),
+                out=grouped[:, PACK * c0 : PACK * c1].rearrange("p (c e i) -> p c i e", e=4, i=PACK),
+                in_=raw[:, :, c0:c1].rearrange("p i (c e) -> p c i e", e=4),
             )
 
         xg, x_grouped, down_pairs, w_grouped, up_pairs = {}, {}, {}, {}, {}
 
-        def both(function, lo, mid, hi):
-            if mid > lo:
-                function(nc.vector.tensor_copy, lo, mid)
-            if hi > mid:
-                function(nc.scalar.copy, mid, hi)
-
-        def pick(a):
-            picked = stage.tile([P, 4, S], F32, name="picked", bufs=2)
-            for i in range(4):
-                for h in range(2):
-                    cols = slice(256 * h, 256 * (h + 1))
+        def pick_x(a):
+            picked = stage.tile([P, PACK, S], F32, name="picked", bufs=2)
+            for i in range(PACK):
+                for j0 in range(0, S, HALF):
+                    j = slice(j0, j0 + HALF)
                     nc.vector.tensor_tensor(
-                        out=picked[:, i, cols],
-                        in0=windows[a, i][:].indirect(lists[:, 16 * h : 16 * (h + 1)]),
-                        in1=weight[:, cols],
+                        out=picked[:, i, j],
+                        in0=windows[a, i][:].indirect(lists[:, j0 // 16 : (j0 + HALF) // 16]),
+                        in1=weight[:, j],
                         op=MULT,
                     )
-            x_grouped[a] = stage.tile([P, 4 * S], BF16, name="x_grouped", align_bytes=64, bufs=3)
-            interleave(nc.scalar.copy, x_grouped[a], picked, 0, S)
+            x_grouped[a] = stage.tile([P, PACK * S], BF16, name="x_grouped", align_bytes=64)
+            shared(lambda copy, c0, c1: interleave(copy, x_grouped[a], picked, c0, c1), 0, X_ON_VECTOR[a], S)
 
         def quantise_x(a):
-            xg[a] = quantised(f"xg{a}", S)
+            xg[a] = quantised(f"xg{a}", S, f"window{a + 1}_{PACK - 1}" if a < PASSES - 1 else None)
             quantise(xg[a], x_grouped[a], 0, S)
+
+        def group_down(a):
+            w_grouped[a] = stage.tile([P, PACK * R], BF16, name="w_grouped", align_bytes=64)
+
+            def part(copy, m0, m1):
+                copy(
+                    out=w_grouped[a][:].rearrange("p (t m i) -> p m t i", t=4, i=PACK)[:, m0:m1, :, :],
+                    in_=down_raw[a][:].rearrange("p i (m t) -> p m t i", t=4)[:, m0:m1, :, :],
+                )
+
+            shared(part, 0, DOWN_ON_VECTOR[a], P)
+
+        def quantise_down(a):
+            down_pairs[a] = quantised(f"down{a}", R)
+            quantise(down_pairs[a], w_grouped[a], 0, R)
+
+        def group_up(c):
+            grouped = stage.tile([P, PACK * UP_COLS], BF16, name="w_grouped", align_bytes=64)
+            w_grouped["up", c] = grouped
+            shared(lambda copy, c0, c1: interleave(copy, grouped, up_raw[c], c0, c1), 0, UP_ON_VECTOR, UP_COLS)
+
+        def quantise_up(c):
+            up_pairs[c] = quantised(f"up{c}", UP_COLS)
+            quantise(up_pairs[c], w_grouped["up", c], 0, UP_COLS)
 
         def w4_passes(a, tiles):
             for m in tiles:
@@ -149,129 +184,90 @@ def tile_list_hlora_bias_kernel(tc, xT, w4_words, w4_scales, down, up, wgt, b, o
                 nc.tensor.matmul_mx(
                     out=y[m][:],
                     lhsT=tile[:, a, 2 * P * mm : 2 * P * (mm + 1)].bitcast(E2M1),
-                    lhsT_scale=w4_planes[:, a, P * m : P * (m + 1)],
+                    lhsT_scale=w4_plane[:, a, P * m : P * (m + 1)],
                     rhs=xg[a][0][:].bitcast(E4M3),
                     rhs_scale=xg[a][1][:],
                     start=(a == 0),
                     stop=False,
                 )
 
-        def group_down(a, share):
-            w_grouped[a] = stage.tile([P, 4 * R], BF16, name="w_grouped", align_bytes=64, bufs=3)
-
-            def part(copy, m0, m1):
-                copy(
-                    out=w_grouped[a][:].rearrange("p (t m j) -> p m t j", t=4, j=4)[:, m0:m1, :, :],
-                    in_=down_raw[a][:].rearrange("p j (m t) -> p m t j", t=4)[:, m0:m1, :, :],
-                )
-
-            both(part, 0, share, P)
-
-        def quantise_down(a):
-            down_pairs[a] = quantised(f"down{a}", R)
-            quantise(down_pairs[a], w_grouped[a], 0, R)
-
         def h_passes(a):
-            codes, plane = down_pairs[a]
             for t in range(4):
-                nc.tensor.matmul_mx(
-                    out=h_acc[t][:],
-                    lhsT=codes[:, P * t : P * (t + 1)].bitcast(E4M3),
-                    lhsT_scale=plane[:, P * t : P * (t + 1)],
-                    rhs=xg[a][0][:].bitcast(E4M3),
-                    rhs_scale=xg[a][1][:],
-                    start=(a == 0),
-                    stop=(a == PASSES - 1),
-                )
-
-        def group_up(c, share):
-            w_grouped["up", c] = stage.tile([P, 4 * 512], BF16, name="w_grouped", align_bytes=64, bufs=3)
-            both(lambda copy, c0, c1: interleave(copy, w_grouped["up", c], up_raw[c], c0, c1), 0, share, 512)
-
-        def quantise_up(c):
-            up_pairs[c] = quantised(f"up{c}", 512)
-            quantise(up_pairs[c], w_grouped["up", c], 0, 512)
-
-        def finish(m):
-            codes, plane = up_pairs[m // 4]
-            cols = slice(P * (m % 4), P * (m % 4 + 1))
-            nc.tensor.matmul_mx(
-                out=y[m][:],
-                lhsT=codes[:, cols].bitcast(E4M3),
-                lhsT_scale=plane[:, cols],
-                rhs=h[0][:].bitcast(E4M3),
-                rhs_scale=h[1][:],
-                start=False,
-                stop=True,
-            )
-            result = outs.tile([P, S], F32, name="result")
-            if m in ON_VECTOR:
-                nc.vector.tensor_scalar(out=result[:], in0=y[m][:], scalar1=b_col[:, m : m + 1], scalar2=None, op0=ADD)
-            else:
-                nc.scalar.activation(result[:], y[m][:], IDENTITY, bias=b_col[:, m : m + 1])
-            nc.sync.dma_start(out[P * m : P * (m + 1), :], result[:])
+                cols = slice(P * t, P * (t + 1))
+                multiply(h_acc[t], down_pairs[a], cols, xg[a], start=(a == 0), stop=(a == PASSES - 1))
 
         def open_tiles(tiles):
             for m in tiles:
-                y[m] = bank((m + 4) % 8)
+                y[m] = bank((m + BANKS - EARLY) % BANKS)
             for a in range(PASSES):
                 w4_passes(a, tiles)
 
-        y = {m: bank(4 + m) for m in range(EARLY)}
+        def finish(m):
+            cols = slice(P * (m % UP_TILES), P * (m % UP_TILES + 1))
+            multiply(y[m], up_pairs[m // UP_TILES], cols, h, start=False, stop=True)
+            result = outs.tile([P, S], F32, name="result")
+            bias = b_col[:, m : m + 1]
+            width = HALF if m == M_TILES - 1 else S
+            for j0 in range(0, S, width):
+                j = slice(j0, j0 + width)
+                if m % 3 == 2:
+                    nc.vector.tensor_scalar(out=result[:, j], in0=y[m][:, j], scalar1=bias, scalar2=None, op0=ADD)
+                else:
+                    nc.scalar.activation(result[:, j], y[m][:, j], IDENTITY, bias=bias)
+                nc.sync.dma_start(out[P * m : P * (m + 1), j], result[:, j])
+
+        early = range(EARLY)
+        y = {m: bank(BANKS - EARLY + m) for m in early}
+        pick_x(0)
+        pick_x(1)
+        b_ps = bank(0)
+        nc.tensor.transpose(b_ps[:, 0:P], b_rows[:], ident[:])
+        b_col = keep.tile([P, M_TILES], F32, name="b_col")
+        nc.vector.tensor_copy(b_col[:], b_ps[:, 0:M_TILES])
         h_acc = [bank(t) for t in range(4)]
-        pick(0)
-        pick(1)
-        group_down(0, 0)
+        group_down(0)
         quantise_x(0)
-        w4_passes(0, range(EARLY))
-        pick(2)
+        w4_passes(0, early)
+        pick_x(2)
         quantise_x(1)
-        w4_passes(1, range(EARLY))
-        pick(3)
+        w4_passes(1, early)
+        pick_x(3)
         quantise_down(0)
         h_passes(0)
         quantise_x(2)
-        w4_passes(2, range(EARLY))
-        group_down(1, P)
+        w4_passes(2, early)
+        group_down(1)
         quantise_down(1)
         h_passes(1)
         quantise_x(3)
-        group_down(2, P)
-        quantise_down(2)
-        h_passes(2)
-        group_down(3, 64)
-        quantise_down(3)
-        h_passes(3)
-        w4_passes(3, range(EARLY))
+        for a in (2, 3):
+            group_down(a)
+            quantise_down(a)
+            h_passes(a)
+        w4_passes(3, early)
 
-        group_up(0, 384)
-        h_planes = keep.tile([P, 4, S], BF16, name="h_planes", align_bytes=64)
-        h_grouped = keep.tile([P, 4 * S], BF16, name="h_grouped", align_bytes=64)
+        group_up(0)
+        h_raw = keep.tile([P, 4, S], BF16, name="h_raw", align_bytes=64)
+        h_grouped = keep.tile([P, PACK * S], BF16, name="h_grouped", align_bytes=64)
         for t in range(4):
             copy = nc.vector.tensor_copy if t == 1 else nc.scalar.copy
-            copy(out=h_planes[:, t, :], in_=h_acc[t][:])
+            copy(out=h_raw[:, t, :], in_=h_acc[t][:])
         quantise_up(0)
-        both(lambda copy, c0, c1: interleave(copy, h_grouped, h_planes, c0, c1), 0, 256, 512)
+        shared(lambda copy, c0, c1: interleave(copy, h_grouped, h_raw, c0, c1), 0, HALF, S)
         h = quantised("h", S)
-        quantise(h, h_grouped, 0, 256)
-        quantise(h, h_grouped, 256, 512)
-        group_up(1, 512)
+        quantise(h, h_grouped, 0, HALF)
+        quantise(h, h_grouped, HALF, S)
+
+        group_up(1)
         open_tiles((4, 5))
-        for m in range(4):
+        for m in early:
             finish(m)
         quantise_up(1)
-        group_up(2, 512)
+        group_up(2)
         open_tiles((6, 7))
-        finish(4)
-        finish(5)
-        open_tiles((8,))
-        finish(6)
-        open_tiles((9,))
-        finish(7)
+        for m in range(4, 8):
+            finish(m)
         quantise_up(2)
-        finish(8)
-        finish(9)
-        open_tiles((10,))
-        finish(10)
-        open_tiles((11,))
-        finish(11)
+        for m in range(8, M_TILES):
+            open_tiles((m,))
+            finish(m)

from contextlib import ExitStack

import concourse.mybir as mybir
from concourse.masks import make_identity

F32 = mybir.dt.float32
BF16 = mybir.dt.bfloat16
I32 = mybir.dt.int32
U32 = mybir.dt.uint32
U16 = mybir.dt.uint16
U8 = mybir.dt.uint8
E4M3 = mybir.dt.float8_e4m3fn_x4
E2M1 = mybir.dt.float4_e2m1fn_x4
ADD = mybir.AluOpType.add
MULT = mybir.AluOpType.mult
IDENTITY = mybir.ActivationFunctionType.Identity

K, R, M, T, S = 2048, 512, 1536, 1024, 512
P = 128
PACK = 4
PASSES = K // (P * PACK)
M_TILES = M // P
HALF = S // 2

BANKS = 8
EARLY = 4
UP_COLS = 512
UP_TILES = UP_COLS // P

X_ON_VECTOR = [0, 0, 0, HALF]
DOWN_ON_VECTOR = [0, 0, 64, 64]
UP_ON_VECTOR = 384

FLOPS = 2 * S * (K * M + K * R + R * M)


def tile_list_hlora_bias_kernel(tc, xT, w4_words, w4_scales, down, up, wgt, b, offs, out):
    nc = tc.nc
    with ExitStack() as ctx:
        keep = ctx.enter_context(tc.tile_pool(name="keep", bufs=1))
        stage = ctx.enter_context(tc.tile_pool(name="stage", bufs=3))
        outs = ctx.enter_context(tc.tile_pool(name="outs", bufs=8))
        psum = ctx.enter_context(tc.psum_pool(name="psum", bufs=1))

        def bank(n):
            return psum.tile([P, S], F32, name=f"bank{n}")

        w4_plane = keep.tile([P, PASSES, M], U8, name="w4_plane", align_bytes=64)
        nc.vector.memset(w4_plane[:].rearrange("p a n -> p (a n)").bitcast(I32), 0)
        b_rows = keep.tile([P, P], F32, name="b_rows")
        nc.gpsimd.memset(b_rows[:], 0.0)
        b_lines = b.rearrange("(m p) -> m p", p=P)
        for first, last in ((0, 8), (8, M_TILES)):
            nc.gpsimd.dma_start(out=b_rows[first:last, :], in_=b_lines[first:last, :])
        for q in range(4):
            nc.gpsimd.dma_start(
                out=w4_plane[32 * q : 32 * q + 4, :, :].bitcast(I32),
                in_=w4_scales[:, 4 * q : 4 * q + 4, :].rearrange("a e n -> e a n").bitcast(I32),
            )
        ident = keep.tile([P, P], F32, name="ident")
        make_identity(nc, ident[:])

        weight = keep.tile([P, S], F32, name="weight")
        lists = keep.tile([P, S // 16], U16, name="lists")
        windows, down_raw, up_raw = {}, {}, {}
        w4_early = keep.tile([P, PASSES, 2 * P * EARLY], U8, name="w4_early", align_bytes=64)
        w4_late = keep.tile([P, PASSES, 2 * P * (M_TILES - EARLY)], U8, name="w4_late", align_bytes=64)

        def load_window(a, i):
            windows[a, i] = keep.tile([P, T], F32, name=f"window{a}_{i}", tag=f"window{a}_{i}", align_bytes=64)
            rows = xT[P * PACK * a : P * PACK * (a + 1), :].rearrange("(p i) t -> p i t", i=PACK)
            nc.sync.dma_start(windows[a, i][:], rows[:, i, :])

        def load_down(a):
            down_raw[a] = keep.tile([P, PACK, R], F32, name=f"down_raw{a}")
            rows = down[P * PACK * a : P * PACK * (a + 1), :]
            nc.sync.dma_start(down_raw[a][:], rows.rearrange("(p i) r -> p i r", i=PACK))

        def load_up(c):
            up_raw[c] = keep.tile([P, PACK, UP_COLS], F32, name=f"up_raw{c}")
            cols = up[:, UP_COLS * c : UP_COLS * (c + 1)]
            nc.sync.dma_start(up_raw[c][:], cols.rearrange("(p i) n -> p i n", i=PACK))

        def load_w4(tile, first, last):
            cols = w4_words[:, :, 2 * P * first : 2 * P * last]
            nc.sync.dma_start(tile[:].bitcast(I32), cols.rearrange("a p n -> p a n").bitcast(I32))

        nc.sync.dma_start(weight[:], wgt)
        nc.sync.dma_start(lists[:], offs)
        for a in range(PASSES):
            for i in range(PACK):
                if a >= 2 and i == 2:
                    load_down(a - 2)
                load_window(a, i)
        load_w4(w4_early, 0, EARLY)
        load_down(2)
        load_down(3)
        load_up(0)
        load_w4(w4_late, EARLY, M_TILES)
        load_up(1)
        load_up(2)

        def quantised(name, width, after=None):
            codes = keep.tile([P, width], U32, name=f"{name}_codes", tag=after or f"{name}_codes", align_bytes=64)
            plane = keep.tile([P, width], U8, name=f"{name}_plane", align_bytes=64)
            return codes, plane

        def quantise(pair, grouped, c0, c1):
            codes, plane = pair
            nc.vector.quantize_mx(
                out=codes[:, c0:c1].bitcast(E4M3), scales=plane[:, c0:c1], in_=grouped[:, PACK * c0 : PACK * c1]
            )

        def multiply(acc, weights, cols, moving, **flags):
            codes, plane = weights
            nc.tensor.matmul_mx(
                out=acc[:],
                lhsT=codes[:, cols].bitcast(E4M3),
                lhsT_scale=plane[:, cols],
                rhs=moving[0][:].bitcast(E4M3),
                rhs_scale=moving[1][:],
                **flags,
            )

        def shared(part, lo, mid, hi):
            if mid > lo:
                part(nc.vector.tensor_copy, lo, mid)
            if hi > mid:
                part(nc.scalar.copy, mid, hi)

        def interleave(copy, grouped, raw, c0, c1):
            copy(
                out=grouped[:, PACK * c0 : PACK * c1].rearrange("p (c e i) -> p c i e", e=4, i=PACK),
                in_=raw[:, :, c0:c1].rearrange("p i (c e) -> p c i e", e=4),
            )

        xg, x_grouped, down_pairs, w_grouped, up_pairs = {}, {}, {}, {}, {}

        def pick_x(a):
            picked = stage.tile([P, PACK, S], F32, name="picked", bufs=2)
            for i in range(PACK):
                for j0 in range(0, S, HALF):
                    j = slice(j0, j0 + HALF)
                    nc.vector.tensor_tensor(
                        out=picked[:, i, j],
                        in0=windows[a, i][:].indirect(lists[:, j0 // 16 : (j0 + HALF) // 16]),
                        in1=weight[:, j],
                        op=MULT,
                    )
            x_grouped[a] = stage.tile([P, PACK * S], BF16, name="x_grouped", align_bytes=64)
            shared(lambda copy, c0, c1: interleave(copy, x_grouped[a], picked, c0, c1), 0, X_ON_VECTOR[a], S)

        def quantise_x(a):
            xg[a] = quantised(f"xg{a}", S, f"window{a + 1}_{PACK - 1}" if a < PASSES - 1 else None)
            quantise(xg[a], x_grouped[a], 0, S)

        def group_down(a):
            w_grouped[a] = stage.tile([P, PACK * R], BF16, name="w_grouped", align_bytes=64)

            def part(copy, m0, m1):
                copy(
                    out=w_grouped[a][:].rearrange("p (t m i) -> p m t i", t=4, i=PACK)[:, m0:m1, :, :],
                    in_=down_raw[a][:].rearrange("p i (m t) -> p m t i", t=4)[:, m0:m1, :, :],
                )

            shared(part, 0, DOWN_ON_VECTOR[a], P)

        def quantise_down(a):
            down_pairs[a] = quantised(f"down{a}", R)
            quantise(down_pairs[a], w_grouped[a], 0, R)

        def group_up(c):
            grouped = stage.tile([P, PACK * UP_COLS], BF16, name="w_grouped", align_bytes=64)
            w_grouped["up", c] = grouped
            shared(lambda copy, c0, c1: interleave(copy, grouped, up_raw[c], c0, c1), 0, UP_ON_VECTOR, UP_COLS)

        def quantise_up(c):
            up_pairs[c] = quantised(f"up{c}", UP_COLS)
            quantise(up_pairs[c], w_grouped["up", c], 0, UP_COLS)

        def w4_passes(a, tiles):
            for m in tiles:
                tile, mm = (w4_early, m) if m < EARLY else (w4_late, m - EARLY)
                nc.tensor.matmul_mx(
                    out=y[m][:],
                    lhsT=tile[:, a, 2 * P * mm : 2 * P * (mm + 1)].bitcast(E2M1),
                    lhsT_scale=w4_plane[:, a, P * m : P * (m + 1)],
                    rhs=xg[a][0][:].bitcast(E4M3),
                    rhs_scale=xg[a][1][:],
                    start=(a == 0),
                    stop=False,
                )

        def h_passes(a):
            for t in range(4):
                cols = slice(P * t, P * (t + 1))
                multiply(h_acc[t], down_pairs[a], cols, xg[a], start=(a == 0), stop=(a == PASSES - 1))

        def open_tiles(tiles):
            for m in tiles:
                y[m] = bank((m + BANKS - EARLY) % BANKS)
            for a in range(PASSES):
                w4_passes(a, tiles)

        def finish(m):
            cols = slice(P * (m % UP_TILES), P * (m % UP_TILES + 1))
            multiply(y[m], up_pairs[m // UP_TILES], cols, h, start=False, stop=True)
            result = outs.tile([P, S], F32, name="result")
            bias = b_col[:, m : m + 1]
            width = HALF if m == M_TILES - 1 else S
            for j0 in range(0, S, width):
                j = slice(j0, j0 + width)
                if m % 3 == 2:
                    nc.vector.tensor_scalar(out=result[:, j], in0=y[m][:, j], scalar1=bias, scalar2=None, op0=ADD)
                else:
                    nc.scalar.activation(result[:, j], y[m][:, j], IDENTITY, bias=bias)
                nc.sync.dma_start(out[P * m : P * (m + 1), j], result[:, j])

        early = range(EARLY)
        y = {m: bank(BANKS - EARLY + m) for m in early}
        pick_x(0)
        pick_x(1)
        b_ps = bank(0)
        nc.tensor.transpose(b_ps[:, 0:P], b_rows[:], ident[:])
        b_col = keep.tile([P, M_TILES], F32, name="b_col")
        nc.vector.tensor_copy(b_col[:], b_ps[:, 0:M_TILES])
        h_acc = [bank(t) for t in range(4)]
        group_down(0)
        quantise_x(0)
        w4_passes(0, early)
        pick_x(2)
        quantise_x(1)
        w4_passes(1, early)
        pick_x(3)
        quantise_down(0)
        h_passes(0)
        quantise_x(2)
        w4_passes(2, early)
        group_down(1)
        quantise_down(1)
        h_passes(1)
        quantise_x(3)
        for a in (2, 3):
            group_down(a)
            quantise_down(a)
            h_passes(a)
        w4_passes(3, early)

        group_up(0)
        h_raw = keep.tile([P, 4, S], BF16, name="h_raw", align_bytes=64)
        h_grouped = keep.tile([P, PACK * S], BF16, name="h_grouped", align_bytes=64)
        for t in range(4):
            copy = nc.vector.tensor_copy if t == 1 else nc.scalar.copy
            copy(out=h_raw[:, t, :], in_=h_acc[t][:])
        quantise_up(0)
        shared(lambda copy, c0, c1: interleave(copy, h_grouped, h_raw, c0, c1), 0, HALF, S)
        h = quantised("h", S)
        quantise(h, h_grouped, 0, HALF)
        quantise(h, h_grouped, HALF, S)

        group_up(1)
        open_tiles((4, 5))
        for m in early:
            finish(m)
        quantise_up(1)
        group_up(2)
        open_tiles((6, 7))
        for m in range(4, 8):
            finish(m)
        quantise_up(2)
        for m in range(8, M_TILES):
            open_tiles((m,))
            finish(m)
